import numpy as np
import ml_dtypes


def mxq(x, axis, fmt="e4m3"):
    dtype, down = {"e4m3": (ml_dtypes.float8_e4m3fn, 7), "e5m2": (ml_dtypes.float8_e5m2, 14)}[fmt]
    v = np.moveaxis(np.asarray(x, np.float32).astype(ml_dtypes.bfloat16).astype(np.float64), axis, -1)
    blocks = v.reshape(v.shape[:-1] + (-1, 32))
    amax = np.abs(blocks).max(-1, keepdims=True)
    byte = np.maximum(np.where(amax > 0, np.frexp(amax)[1] - 1 + 127, 0) - down, 1)
    scale = np.exp2(byte - 127.0)
    codes = (blocks / scale).astype(np.float32).astype(dtype).astype(np.float64)
    return np.moveaxis((codes * scale).reshape(v.shape), -1, axis)


WIDE = False


def mx_kscale(k):
    if not WIDE:
        return np.ones(k)
    levels = np.array([10, -10, 5, -5, 0])
    if k % 512:
        return np.exp2(np.random.permutation(np.resize(levels, k // 32))).repeat(32)
    a = np.empty((k // 512, 16))
    for p in range(k // 512):
        a[p, :8] = np.random.permutation(np.resize(levels, 8))
        for g in range(8):
            far = levels[np.abs(levels - a[p, g]) >= 10]
            a[p, g + 8] = far[np.random.randint(len(far))]
    return np.exp2(a.ravel()).repeat(32)


def f64(x):
    return np.asarray(x).astype(np.float64)


def striped(idx):
    return np.tile(np.asarray(idx).reshape(-1, 16).T, (8, 1)).astype(np.uint16)


def unstriped(offs):
    return offs[:16].T.reshape(-1).astype(np.int64)


E2M1 = np.array([0.0, 0.5, 1.0, 1.5, 2.0, 3.0, 4.0, 6.0, -0.0, -0.5, -1.0, -1.5, -2.0, -3.0, -4.0, -6.0])


def pack_weight(w, fmt):
    k, n = w.shape
    w = f64(np.asarray(w, np.float32).astype(ml_dtypes.bfloat16)).reshape(k // 32, 32, n)
    amax = np.abs(w).max(1)
    if fmt == "e4m3":
        byte = np.frexp(amax)[1] - 1 + 127 - 7
    else:
        mant, ex = np.frexp(amax / 6.0)
        byte = np.where(mant > 0.5, ex, ex - 1) + 127
    byte = np.clip(np.where(amax > 0, byte, 1), 1, 254)
    scaled = (w * np.exp2(127.0 - byte)[:, None, :]).reshape(k, n).astype(np.float32)
    by_word = np.ascontiguousarray(scaled.reshape(k // 512, 128, 4, n).transpose(0, 1, 3, 2))
    if fmt == "e4m3":
        words = by_word.astype(ml_dtypes.float8_e4m3fn).view(np.uint8)
    else:
        c = by_word.astype(ml_dtypes.float4_e2m1fn).view(np.uint8) & 0xF
        words = (c[..., 0::2] | (c[..., 1::2] << 4)).reshape(k // 512, 128, 2 * n)
    return np.ascontiguousarray(words), np.ascontiguousarray(byte.astype(np.uint8).reshape(k // 512, 16, n))


def unpack_weight(words, scales, fmt):
    g, _, n = scales.shape
    words = np.ascontiguousarray(words).reshape(g, 128, n, -1)
    if fmt == "e4m3":
        vals = words.view(ml_dtypes.float8_e4m3fn).astype(np.float64)
    else:
        nib = np.empty((g, 128, n, 4), np.uint8)
        nib[..., 0::2] = words & 0xF
        nib[..., 1::2] = words >> 4
        vals = E2M1[nib]
    vals = vals * np.repeat(np.exp2(scales.astype(np.float64) - 127.0), 8, axis=1)[..., None]
    return vals.transpose(0, 1, 3, 2).reshape(g * 512, n)


B, N, T, D, NQ = 1, 1024, 4096, 512, 128
SEG = 16


def setup_inputs():
    n = np.random.standard_normal
    pages = np.random.permutation(T // 16)[:B * N // 16]
    idx = (pages[:, None] * 16 + np.arange(16)[None, :]).reshape(-1)
    s = mx_kscale(D)[:, None]
    kp = pack_weight(n((D, T)) / s, "e4m3")
    return {
        "qT": (n((B, D, NQ)) * s * (1.00 / np.sqrt(D))).astype(np.float32),
        "k_words": kp[0],
        "k_scales": kp[1],
        "iw": (np.random.uniform(0.2, 2.0, (B, NQ, 1))).astype(np.float32),
        "offs": striped(idx),
    }


def reference(qT, k_words, k_scales, iw, offs):
    idx = unstriped(offs)
    pick = lambda x, which: x[:, which].reshape(x.shape[0], B, -1).transpose(1, 0, 2)
    k = unpack_weight(k_words, k_scales, "e4m3")
    kg = pick(k, idx)
    qq = mxq(f64(qT), 1, "e4m3")
    a = qq.transpose(0, 2, 1) @ kg
    y = a.reshape(B, NQ, N // SEG, SEG).max(-1) * f64(iw)
    return y

@@ -1,0 +1,100 @@
+from contextlib import ExitStack
+
+import concourse.mybir as mybir
+
+F32 = mybir.dt.float32
+BF16 = mybir.dt.bfloat16
+I32 = mybir.dt.int32
+U32 = mybir.dt.uint32
+U16 = mybir.dt.uint16
+U8 = mybir.dt.uint8
+FP8X4 = mybir.dt.float8_e4m3fn_x4
+
+P = 128
+PACK = 4
+T = 4096
+N = 1024
+NQ = 128
+SEG = 16
+HALF = N // 2
+PIECE = 128
+FLOPS = 2 * NQ * P * PACK * N
+
+
+def tile_attend_softmaxsim_kernel(tc, qT, k_words, k_scales, iw, offs, out):
+    nc = tc.nc
+    with ExitStack() as ctx:
+        sb = ctx.enter_context(tc.tile_pool(name="sb", bufs=1))
+        ps = ctx.enter_context(tc.psum_pool(name="ps", bufs=1))
+
+        offsets = sb.tile([P, N // 16], U16, name="offsets")
+        nc.sync.dma_start(offsets[:], offs)
+
+        q_raw = sb.tile([P, PACK, NQ], F32, name="q_raw")
+        nc.scalar.dma_start(out=q_raw[:], in_=qT[0].rearrange("(p j) w -> p j w", j=PACK))
+        pool_words = sb.tile([P, T], U32, name="pool_words", align_bytes=64)
+        nc.scalar.dma_start(
+            out=pool_words[:].bitcast(I32),
+            in_=k_words[0].rearrange("p n t -> p (n t)").bitcast(I32),
+        )
+        weight = sb.tile([P, 1], F32, name="weight")
+        nc.scalar.dma_start(out=weight[:], in_=iw[0])
+
+        pool_scales = sb.tile([P, T], U8, name="pool_scales", align_bytes=64)
+        nc.vector.memset(pool_scales[:].bitcast(I32), 0)
+        nc.sync.dma_start(out=pool_scales[32:96:4, :].bitcast(I32), in_=k_scales[0].bitcast(I32))
+
+        k_plane = sb.tile([P, N], U8, name="k_plane", align_bytes=64)
+        nc.vector.memset(k_plane[:].bitcast(I32), 0)
+        picked_scales = sb.tile([P, N], U8, name="picked_scales", align_bytes=64)
+        nc.vector.tensor_copy(out=picked_scales[:], in_=pool_scales[:].indirect(offsets[:]))
+        for quad in range(4):
+            first = 32 + 16 * quad
+            nc.sync.dma_start(
+                out=k_plane[32 * quad : 32 * quad + 4, :].bitcast(I32),
+                in_=picked_scales[first : first + 16 : 4, :].bitcast(I32),
+            )
+
+        q_bf = sb.tile([P, NQ, PACK], BF16, name="q_bf", align_bytes=64)
+        nc.vector.tensor_copy(out=q_bf[:], in_=q_raw[:].rearrange("p j w -> p w j"))
+        q_codes = sb.tile([P, NQ], U32, name="q_codes", align_bytes=64)
+        q_plane = sb.tile([P, NQ], U8, name="q_plane", align_bytes=64)
+        nc.vector.quantize_mx(
+            out=q_codes[:].bitcast(FP8X4),
+            scales=q_plane[:],
+            in_=q_bf[:].rearrange("p w j -> p (w j)"),
+        )
+
+        picked = []
+        for h in range(2):
+            words = sb.tile([P, HALF], U32, name="picked_words%d" % h, align_bytes=64)
+            cols = slice(h * HALF // 16, (h + 1) * HALF // 16)
+            nc.vector.tensor_copy(out=words[:], in_=pool_words[:].indirect(offsets[:, cols]))
+            picked.append(words)
+
+        best = sb.tile([P, N // SEG], F32, name="best")
+        runs = PIECE // SEG
+        for i in range(N // PIECE):
+            h, at = divmod(i * PIECE, HALF)
+            scores = ps.tile([NQ, PIECE], F32, name="scores%d" % i)
+            nc.tensor.matmul_mx(
+                out=scores[:],
+                lhsT=q_codes[:].bitcast(FP8X4),
+                lhsT_scale=q_plane[:],
+                rhs=picked[h][:, at : at + PIECE].bitcast(FP8X4),
+                rhs_scale=k_plane[:, i * PIECE : (i + 1) * PIECE],
+                start=True,
+                stop=True,
+            )
+            nc.vector.tensor_reduce(
+                out=best[:, i * runs : (i + 1) * runs],
+                in_=scores[:].rearrange("q (j s) -> q j s", s=SEG),
+                axis=mybir.AxisListType.X,
+                op=mybir.AluOpType.max,
+            )
+
+        result = sb.tile([P, N // SEG], F32, name="result")
+        nc.vector.tensor_scalar(
+            out=result[:], in0=best[:], scalar1=weight[:], scalar2=None, op0=mybir.AluOpType.mult
+        )
+        nc.sync.dma_start(out=out[0], in_=result[:])

@@ -36,11 +36,12 @@ def tile_attend_softmaxsim_kernel(tc, qT, k_words, k_scales, iw, offs, out):
         nc.scalar.dma_start(
             out=pool_words[:].bitcast(I32),
             in_=k_words[0].rearrange("p n t -> p (n t)").bitcast(I32),
+            max_dma_last_dim=8192,
         )
         weight = sb.tile([P, 1], F32, name="weight")
         nc.scalar.dma_start(out=weight[:], in_=iw[0])
 
-        pool_scales = sb.tile([P, T], U8, name="pool_scales", align_bytes=64)
+        pool_scales = sb.tile([P, T], U8, name="pool_scales", tag="shared", align_bytes=64)
         nc.vector.memset(pool_scales[:].bitcast(I32), 0)
         nc.sync.dma_start(out=pool_scales[32:96:4, :].bitcast(I32), in_=k_scales[0].bitcast(I32))
 
@@ -55,7 +56,7 @@ def tile_attend_softmaxsim_kernel(tc, qT, k_words, k_scales, iw, offs, out):
                 in_=picked_scales[first : first + 16 : 4, :].bitcast(I32),
             )
 
-        q_bf = sb.tile([P, NQ, PACK], BF16, name="q_bf", align_bytes=64)
+        q_bf = sb.tile([P, NQ, PACK], BF16, name="q_bf", tag="shared", align_bytes=64)
         nc.vector.tensor_copy(out=q_bf[:], in_=q_raw[:].rearrange("p j w -> p w j"))
         q_codes = sb.tile([P, NQ], U32, name="q_codes", align_bytes=64)
         q_plane = sb.tile([P, NQ], U8, name="q_plane", align_bytes=64)
@@ -65,23 +66,22 @@ def tile_attend_softmaxsim_kernel(tc, qT, k_words, k_scales, iw, offs, out):
             in_=q_bf[:].rearrange("p w j -> p (w j)"),
         )
 
-        picked = []
+        picked = sb.tile([P, N], U32, name="picked_words", tag="shared", align_bytes=64)
         for h in range(2):
-            words = sb.tile([P, HALF], U32, name="picked_words%d" % h, align_bytes=64)
             cols = slice(h * HALF // 16, (h + 1) * HALF // 16)
-            nc.vector.tensor_copy(out=words[:], in_=pool_words[:].indirect(offsets[:, cols]))
-            picked.append(words)
+            nc.vector.tensor_copy(
+                out=picked[:, h * HALF : (h + 1) * HALF], in_=pool_words[:].indirect(offsets[:, cols])
+            )
 
         best = sb.tile([P, N // SEG], F32, name="best")
         runs = PIECE // SEG
         for i in range(N // PIECE):
-            h, at = divmod(i * PIECE, HALF)
             scores = ps.tile([NQ, PIECE], F32, name="scores%d" % i)
             nc.tensor.matmul_mx(
                 out=scores[:],
                 lhsT=q_codes[:].bitcast(FP8X4),
                 lhsT_scale=q_plane[:],
-                rhs=picked[h][:, at : at + PIECE].bitcast(FP8X4),
+                rhs=picked[:, i * PIECE : (i + 1) * PIECE].bitcast(FP8X4),
                 rhs_scale=k_plane[:, i * PIECE : (i + 1) * PIECE],
                 start=True,
                 stop=True,

@@ -29,6 +29,8 @@ def tile_attend_softmaxsim_kernel(tc, qT, k_words, k_scales, iw, offs, out):
 
         offsets = sb.tile([P, N // 16], U16, name="offsets")
         nc.sync.dma_start(offsets[:], offs)
+        weight = sb.tile([P, 1], F32, name="weight")
+        nc.sync.dma_start(out=weight[:], in_=iw[0])
 
         q_raw = sb.tile([P, PACK, NQ], F32, name="q_raw")
         nc.scalar.dma_start(out=q_raw[:], in_=qT[0].rearrange("(p j) w -> p j w", j=PACK))
@@ -38,10 +40,11 @@ def tile_attend_softmaxsim_kernel(tc, qT, k_words, k_scales, iw, offs, out):
             in_=k_words[0].rearrange("p n t -> p (n t)").bitcast(I32),
             max_dma_last_dim=8192,
         )
-        weight = sb.tile([P, 1], F32, name="weight")
-        nc.scalar.dma_start(out=weight[:], in_=iw[0])
 
-        pool_scales = sb.tile([P, T], U8, name="pool_scales", tag="shared", align_bytes=64)
+        q_bf = sb.tile([P, NQ, PACK], BF16, name="q_bf", tag="queries_then_keys", align_bytes=64)
+        nc.scalar.copy(out=q_bf[:], in_=q_raw[:].rearrange("p j w -> p w j"))
+
+        pool_scales = sb.tile([P, T], U8, name="pool_scales", tag="scales_then_codes", align_bytes=64)
         nc.vector.memset(pool_scales[:].bitcast(I32), 0)
         nc.sync.dma_start(out=pool_scales[32:96:4, :].bitcast(I32), in_=k_scales[0].bitcast(I32))
 
@@ -51,14 +54,13 @@ def tile_attend_softmaxsim_kernel(tc, qT, k_words, k_scales, iw, offs, out):
         nc.vector.tensor_copy(out=picked_scales[:], in_=pool_scales[:].indirect(offsets[:]))
         for quad in range(4):
             first = 32 + 16 * quad
-            nc.sync.dma_start(
+            queue = nc.sync if quad % 2 == 0 else nc.scalar
+            queue.dma_start(
                 out=k_plane[32 * quad : 32 * quad + 4, :].bitcast(I32),
                 in_=picked_scales[first : first + 16 : 4, :].bitcast(I32),
             )
 
-        q_bf = sb.tile([P, NQ, PACK], BF16, name="q_bf", tag="shared", align_bytes=64)
-        nc.vector.tensor_copy(out=q_bf[:], in_=q_raw[:].rearrange("p j w -> p w j"))
-        q_codes = sb.tile([P, NQ], U32, name="q_codes", align_bytes=64)
+        q_codes = sb.tile([P, NQ], U32, name="q_codes", tag="scales_then_codes", align_bytes=64)
         q_plane = sb.tile([P, NQ], U8, name="q_plane", align_bytes=64)
         nc.vector.quantize_mx(
             out=q_codes[:].bitcast(FP8X4),
@@ -66,7 +68,7 @@ def tile_attend_softmaxsim_kernel(tc, qT, k_words, k_scales, iw, offs, out):
             in_=q_bf[:].rearrange("p w j -> p (w j)"),
         )
 
-        picked = sb.tile([P, N], U32, name="picked_words", tag="shared", align_bytes=64)
+        picked = sb.tile([P, N], U32, name="picked_words", tag="queries_then_keys", align_bytes=64)
         for h in range(2):
             cols = slice(h * HALF // 16, (h + 1) * HALF // 16)
             nc.vector.tensor_copy(

@@ -18,6 +18,7 @@ NQ = 128
 SEG = 16
 HALF = N // 2
 PIECE = 128
+EARLY = 256
 FLOPS = 2 * NQ * P * PACK * N
 
 
@@ -27,19 +28,13 @@ def tile_attend_softmaxsim_kernel(tc, qT, k_words, k_scales, iw, offs, out):
         sb = ctx.enter_context(tc.tile_pool(name="sb", bufs=1))
         ps = ctx.enter_context(tc.psum_pool(name="ps", bufs=1))
 
+        q_raw = sb.tile([P, PACK, NQ], F32, name="q_raw")
+        nc.sync.dma_start(out=q_raw[:], in_=qT[0].rearrange("(p j) w -> p j w", j=PACK))
         offsets = sb.tile([P, N // 16], U16, name="offsets")
         nc.sync.dma_start(offsets[:], offs)
-        weight = sb.tile([P, 1], F32, name="weight")
-        nc.sync.dma_start(out=weight[:], in_=iw[0])
-
-        q_raw = sb.tile([P, PACK, NQ], F32, name="q_raw")
-        nc.scalar.dma_start(out=q_raw[:], in_=qT[0].rearrange("(p j) w -> p j w", j=PACK))
         pool_words = sb.tile([P, T], U32, name="pool_words", align_bytes=64)
-        nc.scalar.dma_start(
-            out=pool_words[:].bitcast(I32),
-            in_=k_words[0].rearrange("p n t -> p (n t)").bitcast(I32),
-            max_dma_last_dim=8192,
-        )
+        words_hbm = k_words[0].rearrange("p n t -> p (n t)").bitcast(I32)
+        nc.sync.dma_start(out=pool_words[:, :EARLY].bitcast(I32), in_=words_hbm[:, :EARLY])
 
         q_bf = sb.tile([P, NQ, PACK], BF16, name="q_bf", tag="queries_then_keys", align_bytes=64)
         nc.scalar.copy(out=q_bf[:], in_=q_raw[:].rearrange("p j w -> p w j"))
@@ -47,6 +42,9 @@ def tile_attend_softmaxsim_kernel(tc, qT, k_words, k_scales, iw, offs, out):
         pool_scales = sb.tile([P, T], U8, name="pool_scales", tag="scales_then_codes", align_bytes=64)
         nc.vector.memset(pool_scales[:].bitcast(I32), 0)
         nc.sync.dma_start(out=pool_scales[32:96:4, :].bitcast(I32), in_=k_scales[0].bitcast(I32))
+        nc.sync.dma_start(
+            out=pool_words[:, EARLY:].bitcast(I32), in_=words_hbm[:, EARLY:], max_dma_last_dim=8192
+        )
 
         k_plane = sb.tile([P, N], U8, name="k_plane", align_bytes=64)
         nc.vector.memset(k_plane[:].bitcast(I32), 0)
@@ -59,6 +57,9 @@ def tile_attend_softmaxsim_kernel(tc, qT, k_words, k_scales, iw, offs, out):
                 out=k_plane[32 * quad : 32 * quad + 4, :].bitcast(I32),
                 in_=picked_scales[first : first + 16 : 4, :].bitcast(I32),
             )
+
+        weight = sb.tile([P, 1], F32, name="weight")
+        nc.sync.dma_start(out=weight[:], in_=iw[0])
 
         q_codes = sb.tile([P, NQ], U32, name="q_codes", tag="scales_then_codes", align_bytes=64)
         q_plane = sb.tile([P, NQ], U8, name="q_plane", align_bytes=64)

@@ -18,7 +18,7 @@ NQ = 128
 SEG = 16
 HALF = N // 2
 PIECE = 128
-EARLY = 256
+EARLY = 640
 FLOPS = 2 * NQ * P * PACK * N
 
 

@@ -52,8 +52,7 @@ def tile_attend_softmaxsim_kernel(tc, qT, k_words, k_scales, iw, offs, out):
         nc.vector.tensor_copy(out=picked_scales[:], in_=pool_scales[:].indirect(offsets[:]))
         for quad in range(4):
             first = 32 + 16 * quad
-            queue = nc.sync if quad % 2 == 0 else nc.scalar
-            queue.dma_start(
+            nc.scalar.dma_start(
                 out=k_plane[32 * quad : 32 * quad + 4, :].bitcast(I32),
                 in_=picked_scales[first : first + 16 : 4, :].bitcast(I32),
             )

@@ -37,7 +37,7 @@ def tile_attend_softmaxsim_kernel(tc, qT, k_words, k_scales, iw, offs, out):
         nc.sync.dma_start(out=pool_words[:, :EARLY].bitcast(I32), in_=words_hbm[:, :EARLY])
 
         q_bf = sb.tile([P, NQ, PACK], BF16, name="q_bf", tag="queries_then_keys", align_bytes=64)
-        nc.scalar.copy(out=q_bf[:], in_=q_raw[:].rearrange("p j w -> p w j"))
+        nc.vector.tensor_copy(out=q_bf[:], in_=q_raw[:].rearrange("p j w -> p w j"))
 
         pool_scales = sb.tile([P, T], U8, name="pool_scales", tag="scales_then_codes", align_bytes=64)
         nc.vector.memset(pool_scales[:].bitcast(I32), 0)

@@ -96,7 +96,18 @@ def tile_attend_softmaxsim_kernel(tc, qT, k_words, k_scales, iw, offs, out):
             )
 
         result = sb.tile([P, N // SEG], F32, name="result")
+        done = N // SEG - runs
         nc.vector.tensor_scalar(
-            out=result[:], in0=best[:], scalar1=weight[:], scalar2=None, op0=mybir.AluOpType.mult
+            out=result[:, :done],
+            in0=best[:, :done],
+            scalar1=weight[:],
+            scalar2=None,
+            op0=mybir.AluOpType.mult,
+        )
+        nc.vector.tensor_tensor(
+            out=result[:, done:],
+            in0=best[:, done:],
+            in1=weight[:].to_broadcast([P, runs]),
+            op=mybir.AluOpType.mult,
         )
         nc.sync.dma_start(out=out[0], in_=result[:])

@@ -18,7 +18,7 @@ NQ = 128
 SEG = 16
 HALF = N // 2
 PIECE = 128
-EARLY = 640
+EARLY = 384
 FLOPS = 2 * NQ * P * PACK * N
 
 
@@ -34,10 +34,13 @@ def tile_attend_softmaxsim_kernel(tc, qT, k_words, k_scales, iw, offs, out):
         nc.sync.dma_start(offsets[:], offs)
         pool_words = sb.tile([P, T], U32, name="pool_words", align_bytes=64)
         words_hbm = k_words[0].rearrange("p n t -> p (n t)").bitcast(I32)
-        nc.sync.dma_start(out=pool_words[:, :EARLY].bitcast(I32), in_=words_hbm[:, :EARLY])
+        early_words = sb.tile([P, EARLY], I32, name="early_words", tag="early_then_plane", align_bytes=64)
+        nc.sync.dma_start(out=early_words[:], in_=words_hbm[:, :EARLY])
 
-        q_bf = sb.tile([P, NQ, PACK], BF16, name="q_bf", tag="queries_then_keys", align_bytes=64)
+        q_bf = sb.tile([P, NQ, PACK], BF16, name="q_bf", align_bytes=64)
         nc.vector.tensor_copy(out=q_bf[:], in_=q_raw[:].rearrange("p j w -> p w j"))
+
+        nc.vector.tensor_copy(out=pool_words[:, :EARLY].bitcast(I32), in_=early_words[:])
 
         pool_scales = sb.tile([P, T], U8, name="pool_scales", tag="scales_then_codes", align_bytes=64)
         nc.vector.memset(pool_scales[:].bitcast(I32), 0)
@@ -61,14 +64,14 @@ def tile_attend_softmaxsim_kernel(tc, qT, k_words, k_scales, iw, offs, out):
         nc.sync.dma_start(out=weight[:], in_=iw[0])
 
         q_codes = sb.tile([P, NQ], U32, name="q_codes", tag="scales_then_codes", align_bytes=64)
-        q_plane = sb.tile([P, NQ], U8, name="q_plane", align_bytes=64)
+        q_plane = sb.tile([P, NQ], U8, name="q_plane", tag="early_then_plane", align_bytes=64)
         nc.vector.quantize_mx(
             out=q_codes[:].bitcast(FP8X4),
             scales=q_plane[:],
             in_=q_bf[:].rearrange("p w j -> p (w j)"),
         )
 
-        picked = sb.tile([P, N], U32, name="picked_words", tag="queries_then_keys", align_bytes=64)
+        picked = sb.tile([P, N], U32, name="picked_words", align_bytes=64)
         for h in range(2):
             cols = slice(h * HALF // 16, (h + 1) * HALF // 16)
             nc.vector.tensor_copy(

@@ -79,6 +79,7 @@ def tile_attend_softmaxsim_kernel(tc, qT, k_words, k_scales, iw, offs, out):
             )
 
         best = sb.tile([P, N // SEG], F32, name="best")
+        first_result = sb.tile([P, HALF // SEG], F32, name="first_result")
         runs = PIECE // SEG
         for i in range(N // PIECE):
             scores = ps.tile([NQ, PIECE], F32, name="scores%d" % i)
@@ -97,20 +98,25 @@ def tile_attend_softmaxsim_kernel(tc, qT, k_words, k_scales, iw, offs, out):
                 axis=mybir.AxisListType.X,
                 op=mybir.AluOpType.max,
             )
+            if i < HALF // PIECE and i % 2 == 1:
+                passages = slice((i - 1) * runs, (i + 1) * runs)
+                nc.gpsimd.tensor_scalar(
+                    out=first_result[:, passages],
+                    in0=best[:, passages],
+                    scalar1=weight[:],
+                    scalar2=0.0,
+                    op0=mybir.AluOpType.mult,
+                    op1=mybir.AluOpType.add,
+                )
+                for queue, rows in ((nc.sync, slice(0, P // 2)), (nc.scalar, slice(P // 2, P))):
+                    queue.dma_start(out=out[0][rows, passages], in_=first_result[rows, passages])
 
-        result = sb.tile([P, N // SEG], F32, name="result")
-        done = N // SEG - runs
-        nc.vector.tensor_scalar(
-            out=result[:, :done],
-            in0=best[:, :done],
-            scalar1=weight[:],
-            scalar2=None,
-            op0=mybir.AluOpType.mult,
-        )
+        done = HALF // SEG
+        result = sb.tile([P, done], F32, name="result")
         nc.vector.tensor_tensor(
-            out=result[:, done:],
+            out=result[:],
             in0=best[:, done:],
-            in1=weight[:].to_broadcast([P, runs]),
+            in1=weight[:].to_broadcast([P, done]),
             op=mybir.AluOpType.mult,
         )
-        nc.sync.dma_start(out=out[0], in_=result[:])
+        nc.sync.dma_start(out=out[0][:, done:], in_=result[:])

@@ -18,7 +18,7 @@ NQ = 128
 SEG = 16
 HALF = N // 2
 PIECE = 128
-EARLY = 384
+EARLY = 256
 FLOPS = 2 * NQ * P * PACK * N
 
 

@@ -19,6 +19,7 @@ SEG = 16
 HALF = N // 2
 PIECE = 128
 EARLY = 256
+GATHERS = (384, 384, 256)
 FLOPS = 2 * NQ * P * PACK * N
 
 
@@ -72,11 +73,13 @@ def tile_attend_softmaxsim_kernel(tc, qT, k_words, k_scales, iw, offs, out):
         )
 
         picked = sb.tile([P, N], U32, name="picked_words", align_bytes=64)
-        for h in range(2):
-            cols = slice(h * HALF // 16, (h + 1) * HALF // 16)
+        first = 0
+        for width in GATHERS:
+            cols = slice(first // 16, (first + width) // 16)
             nc.vector.tensor_copy(
-                out=picked[:, h * HALF : (h + 1) * HALF], in_=pool_words[:].indirect(offsets[:, cols])
+                out=picked[:, first : first + width], in_=pool_words[:].indirect(offsets[:, cols])
             )
+            first = first + width
 
         best = sb.tile([P, N // SEG], F32, name="best")
         first_result = sb.tile([P, HALF // SEG], F32, name="first_result")

@@ -18,7 +18,7 @@ NQ = 128
 SEG = 16
 HALF = N // 2
 PIECE = 128
-EARLY = 256
+EARLY = 128
 GATHERS = (384, 384, 256)
 FLOPS = 2 * NQ * P * PACK * N
 
@@ -54,11 +54,10 @@ def tile_attend_softmaxsim_kernel(tc, qT, k_words, k_scales, iw, offs, out):
         nc.vector.memset(k_plane[:].bitcast(I32), 0)
         picked_scales = sb.tile([P, N], U8, name="picked_scales", align_bytes=64)
         nc.vector.tensor_copy(out=picked_scales[:], in_=pool_scales[:].indirect(offsets[:]))
-        for quad in range(4):
-            first = 32 + 16 * quad
+        for row in range(4):
             nc.scalar.dma_start(
-                out=k_plane[32 * quad : 32 * quad + 4, :].bitcast(I32),
-                in_=picked_scales[first : first + 16 : 4, :].bitcast(I32),
+                out=k_plane[row:P:32, :].bitcast(I32),
+                in_=picked_scales[32 + 4 * row : 96 : 16, :].bitcast(I32),
             )
 
         weight = sb.tile([P, 1], F32, name="weight")
@@ -116,10 +115,11 @@ def tile_attend_softmaxsim_kernel(tc, qT, k_words, k_scales, iw, offs, out):
 
         done = HALF // SEG
         result = sb.tile([P, done], F32, name="result")
-        nc.vector.tensor_tensor(
-            out=result[:],
-            in0=best[:, done:],
-            in1=weight[:].to_broadcast([P, done]),
-            op=mybir.AluOpType.mult,
-        )
+        for first, last in ((0, done - runs), (done - runs, done)):
+            nc.vector.tensor_tensor(
+                out=result[:, first:last],
+                in0=best[:, done + first : done + last],
+                in1=weight[:].to_broadcast([P, last - first]),
+                op=mybir.AluOpType.mult,
+            )
         nc.sync.dma_start(out=out[0][:, done:], in_=result[:])

@@ -46,9 +46,7 @@ def tile_attend_softmaxsim_kernel(tc, qT, k_words, k_scales, iw, offs, out):
         pool_scales = sb.tile([P, T], U8, name="pool_scales", tag="scales_then_codes", align_bytes=64)
         nc.vector.memset(pool_scales[:].bitcast(I32), 0)
         nc.sync.dma_start(out=pool_scales[32:96:4, :].bitcast(I32), in_=k_scales[0].bitcast(I32))
-        nc.sync.dma_start(
-            out=pool_words[:, EARLY:].bitcast(I32), in_=words_hbm[:, EARLY:], max_dma_last_dim=8192
-        )
+        nc.sync.dma_start(out=pool_words[:, EARLY:].bitcast(I32), in_=words_hbm[:, EARLY:])
 
         k_plane = sb.tile([P, N], U8, name="k_plane", align_bytes=64)
         nc.vector.memset(k_plane[:].bitcast(I32), 0)

@@ -18,7 +18,6 @@ NQ = 128
 SEG = 16
 HALF = N // 2
 PIECE = 128
-EARLY = 128
 GATHERS = (384, 384, 256)
 FLOPS = 2 * NQ * P * PACK * N
 
@@ -30,23 +29,18 @@ def tile_attend_softmaxsim_kernel(tc, qT, k_words, k_scales, iw, offs, out):
         ps = ctx.enter_context(tc.psum_pool(name="ps", bufs=1))
 
         q_raw = sb.tile([P, PACK, NQ], F32, name="q_raw")
-        nc.sync.dma_start(out=q_raw[:], in_=qT[0].rearrange("(p j) w -> p j w", j=PACK))
+        q_hbm = qT[0].rearrange("(p j) w -> p j w", j=PACK)
+        for half in (slice(0, PACK // 2), slice(PACK // 2, PACK)):
+            nc.sync.dma_start(out=q_raw[:, half, :], in_=q_hbm[:, half, :])
         offsets = sb.tile([P, N // 16], U16, name="offsets")
         nc.sync.dma_start(offsets[:], offs)
         pool_words = sb.tile([P, T], U32, name="pool_words", align_bytes=64)
         words_hbm = k_words[0].rearrange("p n t -> p (n t)").bitcast(I32)
-        early_words = sb.tile([P, EARLY], I32, name="early_words", tag="early_then_plane", align_bytes=64)
-        nc.sync.dma_start(out=early_words[:], in_=words_hbm[:, :EARLY])
 
-        q_bf = sb.tile([P, NQ, PACK], BF16, name="q_bf", align_bytes=64)
-        nc.vector.tensor_copy(out=q_bf[:], in_=q_raw[:].rearrange("p j w -> p w j"))
-
-        nc.vector.tensor_copy(out=pool_words[:, :EARLY].bitcast(I32), in_=early_words[:])
-
-        pool_scales = sb.tile([P, T], U8, name="pool_scales", tag="scales_then_codes", align_bytes=64)
+        pool_scales = sb.tile([P, T], U8, name="pool_scales", tag="scales_then_queries", align_bytes=64)
         nc.vector.memset(pool_scales[:].bitcast(I32), 0)
         nc.sync.dma_start(out=pool_scales[32:96:4, :].bitcast(I32), in_=k_scales[0].bitcast(I32))
-        nc.sync.dma_start(out=pool_words[:, EARLY:].bitcast(I32), in_=words_hbm[:, EARLY:])
+        nc.sync.dma_start(out=pool_words[:].bitcast(I32), in_=words_hbm)
 
         k_plane = sb.tile([P, N], U8, name="k_plane", align_bytes=64)
         nc.vector.memset(k_plane[:].bitcast(I32), 0)
@@ -61,8 +55,10 @@ def tile_attend_softmaxsim_kernel(tc, qT, k_words, k_scales, iw, offs, out):
         weight = sb.tile([P, 1], F32, name="weight")
         nc.sync.dma_start(out=weight[:], in_=iw[0])
 
-        q_codes = sb.tile([P, NQ], U32, name="q_codes", tag="scales_then_codes", align_bytes=64)
-        q_plane = sb.tile([P, NQ], U8, name="q_plane", tag="early_then_plane", align_bytes=64)
+        q_bf = sb.tile([P, NQ, PACK], BF16, name="q_bf", tag="scales_then_queries", align_bytes=64)
+        nc.vector.tensor_copy(out=q_bf[:], in_=q_raw[:].rearrange("p j w -> p w j"))
+        q_codes = sb.tile([P, NQ], U32, name="q_codes", align_bytes=64)
+        q_plane = sb.tile([P, NQ], U8, name="q_plane", align_bytes=64)
         nc.vector.quantize_mx(
             out=q_codes[:].bitcast(FP8X4),
             scales=q_plane[:],

@@ -18,6 +18,7 @@ NQ = 128
 SEG = 16
 HALF = N // 2
 PIECE = 128
+EARLY = 128
 GATHERS = (384, 384, 256)
 FLOPS = 2 * NQ * P * PACK * N
 
@@ -26,36 +27,39 @@ def tile_attend_softmaxsim_kernel(tc, qT, k_words, k_scales, iw, offs, out):
     nc = tc.nc
     with ExitStack() as ctx:
         sb = ctx.enter_context(tc.tile_pool(name="sb", bufs=1))
+        reused = ctx.enter_context(tc.tile_pool(name="reused", bufs=1))
         ps = ctx.enter_context(tc.psum_pool(name="ps", bufs=1))
 
         q_raw = sb.tile([P, PACK, NQ], F32, name="q_raw")
-        q_hbm = qT[0].rearrange("(p j) w -> p j w", j=PACK)
-        for half in (slice(0, PACK // 2), slice(PACK // 2, PACK)):
-            nc.sync.dma_start(out=q_raw[:, half, :], in_=q_hbm[:, half, :])
+        nc.sync.dma_start(out=q_raw[:], in_=qT[0].rearrange("(p j) w -> p j w", j=PACK))
         offsets = sb.tile([P, N // 16], U16, name="offsets")
         nc.sync.dma_start(offsets[:], offs)
         pool_words = sb.tile([P, T], U32, name="pool_words", align_bytes=64)
         words_hbm = k_words[0].rearrange("p n t -> p (n t)").bitcast(I32)
+        early_words = sb.tile([P, EARLY], I32, name="early_words", align_bytes=64)
+        nc.sync.dma_start(out=early_words[:], in_=words_hbm[:, :EARLY])
 
-        pool_scales = sb.tile([P, T], U8, name="pool_scales", tag="scales_then_queries", align_bytes=64)
+        nc.vector.tensor_copy(out=pool_words[:, :EARLY].bitcast(I32), in_=early_words[:])
+
+        pool_scales = reused.tile([P, T], U8, name="pool_scales", offset=0, align_bytes=64)
         nc.vector.memset(pool_scales[:].bitcast(I32), 0)
         nc.sync.dma_start(out=pool_scales[32:96:4, :].bitcast(I32), in_=k_scales[0].bitcast(I32))
-        nc.sync.dma_start(out=pool_words[:].bitcast(I32), in_=words_hbm)
+        nc.sync.dma_start(out=pool_words[:, EARLY:].bitcast(I32), in_=words_hbm[:, EARLY:])
 
         k_plane = sb.tile([P, N], U8, name="k_plane", align_bytes=64)
         nc.vector.memset(k_plane[:].bitcast(I32), 0)
         picked_scales = sb.tile([P, N], U8, name="picked_scales", align_bytes=64)
         nc.vector.tensor_copy(out=picked_scales[:], in_=pool_scales[:].indirect(offsets[:]))
         for row in range(4):
-            nc.scalar.dma_start(
+            nc.sync.dma_start(
                 out=k_plane[row:P:32, :].bitcast(I32),
                 in_=picked_scales[32 + 4 * row : 96 : 16, :].bitcast(I32),
             )
 
-        weight = sb.tile([P, 1], F32, name="weight")
+        weight = reused.tile([P, 1], F32, name="weight", offset=2 * NQ * PACK, align_bytes=64)
         nc.sync.dma_start(out=weight[:], in_=iw[0])
 
-        q_bf = sb.tile([P, NQ, PACK], BF16, name="q_bf", tag="scales_then_queries", align_bytes=64)
+        q_bf = reused.tile([P, NQ, PACK], BF16, name="q_bf", offset=0, align_bytes=64)
         nc.vector.tensor_copy(out=q_bf[:], in_=q_raw[:].rearrange("p j w -> p w j"))
         q_codes = sb.tile([P, NQ], U32, name="q_codes", align_bytes=64)
         q_plane = sb.tile([P, NQ], U8, name="q_plane", align_bytes=64)

@@ -51,12 +51,12 @@ def tile_attend_softmaxsim_kernel(tc, qT, k_words, k_scales, iw, offs, out):
         picked_scales = sb.tile([P, N], U8, name="picked_scales", align_bytes=64)
         nc.vector.tensor_copy(out=picked_scales[:], in_=pool_scales[:].indirect(offsets[:]))
         for row in range(4):
-            nc.sync.dma_start(
+            nc.scalar.dma_start(
                 out=k_plane[row:P:32, :].bitcast(I32),
                 in_=picked_scales[32 + 4 * row : 96 : 16, :].bitcast(I32),
             )
 
-        weight = reused.tile([P, 1], F32, name="weight", offset=2 * NQ * PACK, align_bytes=64)
+        weight = sb.tile([P, 1], F32, name="weight")
         nc.sync.dma_start(out=weight[:], in_=iw[0])
 
         q_bf = reused.tile([P, NQ, PACK], BF16, name="q_bf", offset=0, align_bytes=64)

from contextlib import ExitStack

import concourse.mybir as mybir

F32 = mybir.dt.float32
BF16 = mybir.dt.bfloat16
I32 = mybir.dt.int32
U32 = mybir.dt.uint32
U16 = mybir.dt.uint16
U8 = mybir.dt.uint8
FP8X4 = mybir.dt.float8_e4m3fn_x4

P = 128
PACK = 4
T = 4096
N = 1024
NQ = 128
SEG = 16
HALF = N // 2
PIECE = 128
EARLY = 128
GATHERS = (384, 384, 256)
FLOPS = 2 * NQ * P * PACK * N


def tile_attend_softmaxsim_kernel(tc, qT, k_words, k_scales, iw, offs, out):
    nc = tc.nc
    with ExitStack() as ctx:
        sb = ctx.enter_context(tc.tile_pool(name="sb", bufs=1))
        reused = ctx.enter_context(tc.tile_pool(name="reused", bufs=1))
        ps = ctx.enter_context(tc.psum_pool(name="ps", bufs=1))

        q_raw = sb.tile([P, PACK, NQ], F32, name="q_raw")
        nc.sync.dma_start(out=q_raw[:], in_=qT[0].rearrange("(p j) w -> p j w", j=PACK))
        offsets = sb.tile([P, N // 16], U16, name="offsets")
        nc.sync.dma_start(offsets[:], offs)
        pool_words = sb.tile([P, T], U32, name="pool_words", align_bytes=64)
        words_hbm = k_words[0].rearrange("p n t -> p (n t)").bitcast(I32)
        early_words = sb.tile([P, EARLY], I32, name="early_words", align_bytes=64)
        nc.sync.dma_start(out=early_words[:], in_=words_hbm[:, :EARLY])

        nc.vector.tensor_copy(out=pool_words[:, :EARLY].bitcast(I32), in_=early_words[:])

        pool_scales = reused.tile([P, T], U8, name="pool_scales", offset=0, align_bytes=64)
        nc.vector.memset(pool_scales[:].bitcast(I32), 0)
        nc.sync.dma_start(out=pool_scales[32:96:4, :].bitcast(I32), in_=k_scales[0].bitcast(I32))
        nc.sync.dma_start(out=pool_words[:, EARLY:].bitcast(I32), in_=words_hbm[:, EARLY:])

        k_plane = sb.tile([P, N], U8, name="k_plane", align_bytes=64)
        nc.vector.memset(k_plane[:].bitcast(I32), 0)
        picked_scales = sb.tile([P, N], U8, name="picked_scales", align_bytes=64)
        nc.vector.tensor_copy(out=picked_scales[:], in_=pool_scales[:].indirect(offsets[:]))
        for row in range(4):
            nc.scalar.dma_start(
                out=k_plane[row:P:32, :].bitcast(I32),
                in_=picked_scales[32 + 4 * row : 96 : 16, :].bitcast(I32),
            )

        weight = sb.tile([P, 1], F32, name="weight")
        nc.sync.dma_start(out=weight[:], in_=iw[0])

        q_bf = reused.tile([P, NQ, PACK], BF16, name="q_bf", offset=0, align_bytes=64)
        nc.vector.tensor_copy(out=q_bf[:], in_=q_raw[:].rearrange("p j w -> p w j"))
        q_codes = sb.tile([P, NQ], U32, name="q_codes", align_bytes=64)
        q_plane = sb.tile([P, NQ], U8, name="q_plane", align_bytes=64)
        nc.vector.quantize_mx(
            out=q_codes[:].bitcast(FP8X4),
            scales=q_plane[:],
            in_=q_bf[:].rearrange("p w j -> p (w j)"),
        )

        picked = sb.tile([P, N], U32, name="picked_words", align_bytes=64)
        first = 0
        for width in GATHERS:
            cols = slice(first // 16, (first + width) // 16)
            nc.vector.tensor_copy(
                out=picked[:, first : first + width], in_=pool_words[:].indirect(offsets[:, cols])
            )
            first = first + width

        best = sb.tile([P, N // SEG], F32, name="best")
        first_result = sb.tile([P, HALF // SEG], F32, name="first_result")
        runs = PIECE // SEG
        for i in range(N // PIECE):
            scores = ps.tile([NQ, PIECE], F32, name="scores%d" % i)
            nc.tensor.matmul_mx(
                out=scores[:],
                lhsT=q_codes[:].bitcast(FP8X4),
                lhsT_scale=q_plane[:],
                rhs=picked[:, i * PIECE : (i + 1) * PIECE].bitcast(FP8X4),
                rhs_scale=k_plane[:, i * PIECE : (i + 1) * PIECE],
                start=True,
                stop=True,
            )
            nc.vector.tensor_reduce(
                out=best[:, i * runs : (i + 1) * runs],
                in_=scores[:].rearrange("q (j s) -> q j s", s=SEG),
                axis=mybir.AxisListType.X,
                op=mybir.AluOpType.max,
            )
            if i < HALF // PIECE and i % 2 == 1:
                passages = slice((i - 1) * runs, (i + 1) * runs)
                nc.gpsimd.tensor_scalar(
                    out=first_result[:, passages],
                    in0=best[:, passages],
                    scalar1=weight[:],
                    scalar2=0.0,
                    op0=mybir.AluOpType.mult,
                    op1=mybir.AluOpType.add,
                )
                for queue, rows in ((nc.sync, slice(0, P // 2)), (nc.scalar, slice(P // 2, P))):
                    queue.dma_start(out=out[0][rows, passages], in_=first_result[rows, passages])

        done = HALF // SEG
        result = sb.tile([P, done], F32, name="result")
        for first, last in ((0, done - runs), (done - runs, done)):
            nc.vector.tensor_tensor(
                out=result[:, first:last],
                in0=best[:, done + first : done + last],
                in1=weight[:].to_broadcast([P, last - first]),
                op=mybir.AluOpType.mult,
            )
        nc.sync.dma_start(out=out[0][:, done:], in_=result[:])
